import numpy as np
import ml_dtypes


def mxq(x, axis, fmt="e4m3"):
    dtype, down = {"e4m3": (ml_dtypes.float8_e4m3fn, 7), "e5m2": (ml_dtypes.float8_e5m2, 14)}[fmt]
    v = np.moveaxis(np.asarray(x, np.float32).astype(ml_dtypes.bfloat16).astype(np.float64), axis, -1)
    blocks = v.reshape(v.shape[:-1] + (-1, 32))
    amax = np.abs(blocks).max(-1, keepdims=True)
    byte = np.maximum(np.where(amax > 0, np.frexp(amax)[1] - 1 + 127, 0) - down, 1)
    scale = np.exp2(byte - 127.0)
    codes = (blocks / scale).astype(np.float32).astype(dtype).astype(np.float64)
    return np.moveaxis((codes * scale).reshape(v.shape), -1, axis)


WIDE = False


def mx_kscale(k):
    if not WIDE:
        return np.ones(k)
    levels = np.array([10, -10, 5, -5, 0])
    if k % 512:
        return np.exp2(np.random.permutation(np.resize(levels, k // 32))).repeat(32)
    a = np.empty((k // 512, 16))
    for p in range(k // 512):
        a[p, :8] = np.random.permutation(np.resize(levels, 8))
        for g in range(8):
            far = levels[np.abs(levels - a[p, g]) >= 10]
            a[p, g + 8] = far[np.random.randint(len(far))]
    return np.exp2(a.ravel()).repeat(32)


BF16 = ml_dtypes.bfloat16


def bf(x):
    return np.asarray(x, np.float32).astype(BF16)


def f64(x):
    return np.asarray(x).astype(np.float64)


E2M1 = np.array([0.0, 0.5, 1.0, 1.5, 2.0, 3.0, 4.0, 6.0, -0.0, -0.5, -1.0, -1.5, -2.0, -3.0, -4.0, -6.0])


def pack_weight(w, fmt):
    k, n = w.shape
    w = f64(bf(w)).reshape(k // 32, 32, n)
    amax = np.abs(w).max(1)
    if fmt == "e4m3":
        byte = np.frexp(amax)[1] - 1 + 127 - 7
    else:
        mant, ex = np.frexp(amax / 6.0)
        byte = np.where(mant > 0.5, ex, ex - 1) + 127
    byte = np.clip(np.where(amax > 0, byte, 1), 1, 254)
    scaled = (w * np.exp2(127.0 - byte)[:, None, :]).reshape(k, n).astype(np.float32)
    by_word = np.ascontiguousarray(scaled.reshape(k // 512, 128, 4, n).transpose(0, 1, 3, 2))
    if fmt == "e4m3":
        words = by_word.astype(ml_dtypes.float8_e4m3fn).view(np.uint8)
    else:
        c = by_word.astype(ml_dtypes.float4_e2m1fn).view(np.uint8) & 0xF
        words = c[..., 0::2] | (c[..., 1::2] << 4)
    return np.ascontiguousarray(words), np.ascontiguousarray(byte.astype(np.uint8).reshape(k // 512, 16, n))


def unpack_weight(words, scales, fmt):
    g, p, n, _ = words.shape
    if fmt == "e4m3":
        vals = np.ascontiguousarray(words).view(ml_dtypes.float8_e4m3fn).astype(np.float64)
    else:
        nib = np.empty((g, p, n, 4), np.uint8)
        nib[..., 0::2] = words & 0xF
        nib[..., 1::2] = words >> 4
        vals = E2M1[nib]
    vals = vals * np.repeat(np.exp2(scales.astype(np.float64) - 127.0), 8, axis=1)[..., None]
    return vals.transpose(0, 1, 3, 2).reshape(g * 512, n)


B, E, Z, R, H = 1024, 512, 512, 512, 512
G4 = 4 * H
G8 = 8 * H


def sigmoid(v):
    return 1.0 / (1.0 + np.exp(-v))


def draw0():
    s, t, u = mx_kscale(E), mx_kscale(Z), mx_kscale(R)
    hh = bf(np.random.standard_normal((B, E)) * s)
    h = bf(np.random.standard_normal((B, R)) * u)
    c = bf(np.random.standard_normal((B, H)))
    wz_words, wz_scales = pack_weight(np.random.standard_normal((E, Z)) / np.sqrt(E) / s[:, None] * t, "e4m3")
    bz = bf(0.3 * np.random.standard_normal(Z) * t)
    wd_words, wd_scales = pack_weight(np.random.standard_normal((Z, G8)) / np.sqrt(Z) / t[:, None], "e4m3")
    wh_words, wh_scales = pack_weight(np.random.standard_normal((R, G4)) / np.sqrt(R) / u[:, None], "e4m3")
    return {
        "hh": hh,
        "h": h,
        "c": c,
        "wz_words": wz_words,
        "wz_scales": wz_scales,
        "bz": bz,
        "wd_words": wd_words,
        "wd_scales": wd_scales,
        "wh_words": wh_words,
        "wh_scales": wh_scales,
    }


def generate_scale_and_bias(hh, wz, bz, wd, n_gates):
    z = (mxq(hh, 1, "e4m3") @ wz) + bz
    q = mxq(z, 1, "e4m3") @ wd
    return q[:, :n_gates], q[:, n_gates:]


def lstm_update(p, c):
    pi, pg, pf, po = np.split(p, 4, axis=-1)
    c1 = sigmoid(pf + 1.0) * c + sigmoid(pi) * np.tanh(pg)
    h1 = sigmoid(po) * np.tanh(c1)
    return h1, c1


def core(hh, h, c, wz_words, wz_scales, bz, wd_words, wd_scales, wh_words, wh_scales):
    wz = unpack_weight(wz_words, wz_scales, "e4m3")
    wd = unpack_weight(wd_words, wd_scales, "e4m3")
    wh = unpack_weight(wh_words, wh_scales, "e4m3")
    d, beta = generate_scale_and_bias(f64(hh), wz, f64(bz), wd, wh.shape[1])
    r = mxq(f64(h), 1, "e4m3") @ wh
    p = (1.0 + d) * r + beta
    h1, c1 = lstm_update(p, f64(c))
    return h1, c1


def e4m3fn_bytes(y):
    return np.clip(np.asarray(y, np.float64), -448.0, 448.0).astype(np.float32).astype(ml_dtypes.float8_e4m3fn).view(np.uint8)


def e4m3fn_values(b):
    return np.asarray(b, np.uint8).view(ml_dtypes.float8_e4m3fn).astype(np.float64)


def setup_inputs():
    d = draw0()
    x0 = np.asarray(d['hh']).astype(np.float64)
    s = (np.max(np.abs(x0), axis=(0,), keepdims=True) / 448.0).astype(np.float32)
    out = {}
    for k, v in d.items():
        if k == 'hh':
            out['hh_bytes'] = e4m3fn_bytes(x0 / s.astype(np.float64))
            out['hh_scale'] = s
        else:
            out[k] = v
    return out


def reference(hh_bytes, hh_scale, h, c, wz_words, wz_scales, bz, wd_words, wd_scales, wh_words, wh_scales):
    return core(e4m3fn_values(hh_bytes) * hh_scale.astype(np.float64), h, c, wz_words, wz_scales, bz, wd_words, wd_scales, wh_words, wh_scales)

@@ -1,0 +1,405 @@
+from contextlib import ExitStack
+
+import concourse.mybir as mybir
+from concourse.masks import make_identity
+
+F32 = mybir.dt.float32
+BF16 = mybir.dt.bfloat16
+I32 = mybir.dt.int32
+U32 = mybir.dt.uint32
+U8 = mybir.dt.uint8
+FP8 = mybir.dt.float8_e4m3fn
+FP8X4 = mybir.dt.float8_e4m3fn_x4
+ALU = mybir.AluOpType
+ACT = mybir.ActivationFunctionType
+
+B, K, H = 1024, 512, 512
+P = 128
+TILES = B // P
+PAIRS = TILES // 2
+GATE_I, GATE_G, GATE_F, GATE_O = range(4)
+GATE_ORDER = (GATE_F, GATE_I, GATE_G, GATE_O)
+R_AHEAD = 4
+RAMP = 4
+TANH_LAG = 5
+PAIRS_IN = ((0, 1), (2, 3), (4, 5), (6, 7))
+UNITS = ((0,), (1,), (2, 3), (4, 5), (6, 7))
+GROUPS = ((0, 1), (2, 3), (4, 5), (6, 7))
+
+FLOPS = 2 * B * K * (K + 8 * H + 4 * H)
+
+
+def tile_hyperlstmgeneratedscalebiasstep_w8_kernel(
+    tc, hh_bytes, hh_scale, h, c, wz_words, wz_scales, bz, wd_words, wd_scales, wh_words, wh_scales, out_0, out_1
+):
+    nc = tc.nc
+
+    def rows_of(x):
+        return x.rearrange("(p t) n -> p t n", t=TILES)
+
+    def words_of(w):
+        return w[0].rearrange("p n t -> p (n t)").bitcast(I32)
+
+    with ExitStack() as ctx:
+        keep = ctx.enter_context(tc.tile_pool(name="keep", bufs=1))
+        work = ctx.enter_context(tc.tile_pool(name="work", bufs=2))
+        psum = ctx.enter_context(tc.psum_pool(name="psum", bufs=2))
+        ctx.enter_context(tc.manual_schedule())
+
+        def bank(role):
+            return psum.tile([P, 512], F32, name=role)
+
+        def per_unit(name, width, dtype):
+            return {
+                u: keep.tile([P, len(u) * width], dtype, name="%s%d" % (name, u[0]), align_bytes=64) for u in UNITS
+            }
+
+        hh_sb = {pair: keep.tile([P, 2 * K], U8, name="hh_sb%d" % pair[0]) for pair in PAIRS_IN}
+        h_sb = {pair: keep.tile([P, 2 * K], BF16, name="h_sb%d" % pair[0]) for pair in PAIRS_IN}
+
+        def loaded(tiles, u):
+            j = u[0] % 2
+            return tiles[PAIRS_IN[u[0] // 2]][:, K * j : K * (j + len(u))]
+
+        c_sb = {grp: keep.tile([P, len(grp) * H], BF16, name="c_sb%d" % grp[0]) for grp in GROUPS}
+        hh_q, hh_qs = per_unit("hh_q", P, U32), per_unit("hh_qs", P, U8)
+        h_q, h_qs = per_unit("h_q", P, U32), per_unit("h_qs", P, U8)
+        z_q, z_qs = per_unit("z_q", P, U32), per_unit("z_qs", P, U8)
+        unit_of = {tile: u for u in UNITS for tile in u}
+        group_of = {tile: grp for grp in GROUPS for tile in grp}
+        wz_raw = keep.tile([P, K], U32, name="wz_raw")
+        wz_raw_sc = keep.tile([P, K], U8, name="wz_raw_sc")
+        wz = keep.tile([P, K], U32, name="wz", align_bytes=64)
+        wz_sc = keep.tile([P, K], U8, name="wz_sc", align_bytes=64)
+        wh = [keep.tile([P, H], U32, name="wh%d" % g, align_bytes=64) for g in range(4)]
+        wd = [keep.tile([P, 2, H], U32, name="wd%d" % g, align_bytes=64) for g in range(4)]
+        wh_sc = keep.tile([P, H], U8, name="wh_sc", align_bytes=64)
+        wd_sc = keep.tile([P, 2 * H], U8, name="wd_sc", align_bytes=64)
+        hs = keep.tile([P, 4], F32, name="hs")
+        bz_sb = keep.tile([P, 4], BF16, name="bz_sb")
+        ident = keep.tile([P, P], F32, name="ident")
+        warm = keep.tile([P, 1], F32, name="warm")
+
+        nc.vector.memset(warm[:], 0.0)
+        nc.vector.memset(wz_raw_sc[:].bitcast(I32), 0)
+        nc.vector.memset(wh_sc[:].bitcast(I32), 0)
+        nc.vector.memset(wd_sc[:].bitcast(I32), 0)
+        nc.scalar.activation(out=warm[:], in_=warm[:], func=ACT.Sigmoid)
+        nc.gpsimd.dma_start(out=hs[:], in_=hh_scale.rearrange("o (p t) -> p (o t)", t=4))
+        nc.gpsimd.dma_start(out=bz_sb[:], in_=bz.rearrange("(p t) -> p t", t=4))
+        make_identity(nc, ident[:])
+
+        def rows(x, tiles):
+            return rows_of(x)[:, tiles[0] : tiles[-1] + 1, :].rearrange("p t n -> p (t n)")
+
+        def load_rows(dst, src, u):
+            nc.sync.dma_start(out=dst[u][:], in_=rows(src, u))
+
+        def load_scales(dst, src, planes):
+            scale_rows = src[0].bitcast(I32)
+            for quad in range(4):
+                nc.sync.dma_start(
+                    out=dst[32 * quad : 32 * quad + 4 * planes, :].bitcast(I32),
+                    in_=scale_rows[4 * quad : 4 * quad + 4, :].rearrange("r (c n) -> c r n", c=planes),
+                )
+
+        def load_gate(g):
+            nc.sync.dma_start(out=wh[g][:].bitcast(I32), in_=words_of(wh_words)[:, H * g : H * (g + 1)])
+            both = words_of(wd_words).rearrange("p (a g n) -> p a g n", a=2, g=4)
+            nc.sync.dma_start(out=wd[g][:].bitcast(I32), in_=both[:, :, g, :])
+
+        load_rows(hh_sb, hh_bytes, PAIRS_IN[0])
+        nc.sync.dma_start(out=wz_raw[:].bitcast(I32), in_=words_of(wz_words))
+        load_scales(wz_raw_sc, wz_scales, 1)
+        load_rows(h_sb, h, PAIRS_IN[0])
+        load_rows(hh_sb, hh_bytes, PAIRS_IN[1])
+        load_gate(GATE_ORDER[0])
+        load_scales(wh_sc, wh_scales, 4)
+        load_scales(wd_sc, wd_scales, 4)
+        load_rows(h_sb, h, PAIRS_IN[1])
+        load_gate(GATE_ORDER[1])
+        load_rows(hh_sb, hh_bytes, PAIRS_IN[2])
+        load_rows(c_sb, c, GROUPS[0])
+        load_gate(GATE_ORDER[2])
+        load_gate(GATE_ORDER[3])
+        load_rows(h_sb, h, PAIRS_IN[2])
+        load_rows(hh_sb, hh_bytes, PAIRS_IN[3])
+        load_rows(h_sb, h, PAIRS_IN[3])
+        for grp in GROUPS[1:]:
+            load_rows(c_sb, c, grp)
+
+        staged = {}
+
+        def widen_hh(u):
+            wide = work.tile([P, len(u) * K], BF16, name="hh_wide")
+            nc.scalar.copy(out=wide[:], in_=loaded(hh_sb, u).bitcast(FP8))
+            staged["wide", u] = wide
+
+        def turn(src, u):
+            words = src.bitcast(F32)
+            dst = bank("prep")
+            for half in range(2):
+                for j in range(len(u)):
+                    col = P * (len(u) * half + j)
+                    nc.tensor.transpose(dst[:, col : col + P], words[:, 256 * j + half : 256 * (j + 1) : 2], ident[:])
+            return dst[:, : 2 * P * len(u)]
+
+        def turn_hh(u):
+            staged["hh_bank", u] = turn(staged["wide", u][:], u)
+
+        def turn_h(u):
+            staged["h_bank", u] = turn(loaded(h_sb, u), u)
+
+        def scale_hh(u):
+            dst = work.tile([P, len(u) * K], BF16, name="hh_t", align_bytes=64)
+            nc.vector.tensor_tensor(
+                out=dst[:].rearrange("p (n a e) -> p n a e", a=2, e=2),
+                in0=staged["hh_bank", u].bitcast(BF16).rearrange("p (a n e) -> p n a e", a=2, e=2),
+                in1=hs[:].rearrange("p (a e) -> p a e", a=2).unsqueeze(1).to_broadcast([P, len(u) * P, 2, 2]),
+                op=ALU.mult,
+            )
+            staged["hh_t", u] = dst
+
+        def copy_h(u):
+            dst = work.tile([P, len(u) * K], BF16, name="h_t", align_bytes=64)
+            nc.scalar.copy(
+                out=dst[:].bitcast(F32).rearrange("p (n a) -> p n a", a=2),
+                in_=staged["h_bank", u].rearrange("p (a n) -> p n a", a=2),
+            )
+            staged["h_t", u] = dst
+
+        def quantize(name, codes, scales, u):
+            nc.vector.quantize_mx(out=codes[u][:].bitcast(FP8X4), scales=scales[u][:], in_=staged[name, u][:])
+
+        def multiply_z(u, j):
+            dst = bank("prep")
+            cols = slice(P * j, P * (j + 1))
+            for t in range(4):
+                chans = slice(P * t, P * (t + 1))
+                nc.tensor.matmul_mx(
+                    out=dst[:, chans],
+                    lhsT=wz[:, chans].bitcast(FP8X4),
+                    lhsT_scale=wz_sc[:, chans],
+                    rhs=hh_q[u][:, cols].bitcast(FP8X4),
+                    rhs_scale=hh_qs[u][:, cols],
+                    start=True,
+                    stop=True,
+                )
+            staged["z_bank", u, j] = dst
+
+        def bias_z(u, j):
+            if j == 0:
+                staged["z_t", u] = work.tile([P, len(u) * K], BF16, name="z_t", align_bytes=64)
+            nc.vector.tensor_tensor(
+                out=staged["z_t", u][:, K * j : K * (j + 1)].rearrange("p (n t) -> p n t", t=4),
+                in0=staged["z_bank", u, j][:].rearrange("p (t n) -> p n t", t=4),
+                in1=bz_sb[:].unsqueeze(1).to_broadcast([P, P, 4]),
+                op=ALU.add,
+            )
+
+        chunks = [(tile, g) for grp in GROUPS for g in GATE_ORDER for tile in grp]
+
+        def gate_matmul(role, codes, scales, tile, weights, weight_scales):
+            u = unit_of[tile]
+            cols = slice(P * (tile - u[0]), P * (tile - u[0] + 1))
+            dst = bank(role)
+            nc.tensor.matmul_mx(
+                out=dst[:],
+                lhsT=codes[u][:, cols].bitcast(FP8X4),
+                lhsT_scale=scales[u][:, cols],
+                rhs=weights.bitcast(FP8X4),
+                rhs_scale=weight_scales,
+                start=True,
+                stop=True,
+            )
+            return dst
+
+        def wd_scales_of(first_col):
+            plane, col = divmod(first_col, 2 * H)
+            return wd_sc[4 * plane :, col : col + H]
+
+        def recurrent(n):
+            tile, g = chunks[n]
+            src = gate_matmul("r_bank", h_q, h_qs, tile, wh[g][:], wh_sc[4 * g :, :])
+            r = work.tile([P, H], F32, name="r", bufs=R_AHEAD + 2)
+            nc.scalar.copy(out=r[:], in_=src[:])
+            staged["r", n] = r
+
+        def pre_slice(n):
+            tile, g = chunks[n]
+            grp = group_of[tile]
+            if ("pre", grp, g) not in staged:
+                staged["pre", grp, g] = work.tile([P, len(grp) * H], F32, name="pre", bufs=4)
+            j = tile - grp[0]
+            return staged["pre", grp, g][:, H * j : H * (j + 1)]
+
+        def modulate(n):
+            tile, g = chunks[n]
+            d = gate_matmul("d_bank", z_q, z_qs, tile, wd[g][:, 0, :], wd_scales_of(H * g))
+            nc.vector.scalar_tensor_tensor(
+                out=pre_slice(n), in0=d[:], scalar=1.0, in1=staged["r", n][:], op0=ALU.add, op1=ALU.mult
+            )
+
+        def shift(n):
+            tile, g = chunks[n]
+            beta = gate_matmul("beta_bank", z_q, z_qs, tile, wd[g][:, 1, :], wd_scales_of(4 * H + H * g))
+            if g == GATE_F:
+                nc.vector.scalar_tensor_tensor(
+                    out=pre_slice(n), in0=beta[:], scalar=1.0, in1=pre_slice(n), op0=ALU.add, op1=ALU.add
+                )
+            else:
+                nc.vector.tensor_tensor(out=pre_slice(n), in0=beta[:], in1=pre_slice(n), op=ALU.add)
+
+        def span(grp, part):
+            return slice(H * (part[0] - grp[0]), H * (part[-1] - grp[0] + 1))
+
+        def shared(name, grp):
+            if (name, grp) not in staged:
+                staged[name, grp] = work.tile([P, len(grp) * H], F32, name=name)
+            return staged[name, grp]
+
+        def activate(grp, g, part):
+            cols = span(grp, part)
+            nc.scalar.activation(
+                out=shared("gate%d" % g, grp)[:, cols],
+                in_=staged["pre", grp, g][:, cols],
+                func=ACT.Tanh if g == GATE_G else ACT.Sigmoid,
+            )
+
+        def forget(grp, eng):
+            eng.tensor_tensor(
+                out=shared("kept", grp)[:], in0=shared("gate%d" % GATE_F, grp)[:], in1=c_sb[grp][:], op=ALU.mult
+            )
+
+        def candidate(grp, part, eng):
+            cols = span(grp, part)
+            gate = shared("gate%d" % GATE_G, grp)[:, cols]
+            eng.tensor_tensor(out=gate, in0=gate, in1=shared("gate%d" % GATE_I, grp)[:, cols], op=ALU.mult)
+
+        def cell(grp, part, eng):
+            cols = span(grp, part)
+            c1 = shared("c1", grp)[:, cols]
+            eng.tensor_tensor(
+                out=c1, in0=shared("gate%d" % GATE_G, grp)[:, cols], in1=shared("kept", grp)[:, cols], op=ALU.add
+            )
+            nc.sync.dma_start(out=rows(out_1, part), in_=c1)
+
+        def squash(grp, part):
+            cols = span(grp, part)
+            nc.scalar.activation(out=shared("squashed", grp)[:, cols], in_=shared("c1", grp)[:, cols], func=ACT.Tanh)
+
+        def hidden(grp, part, eng):
+            cols = span(grp, part)
+            h1 = shared("h1", grp)[:, cols]
+            eng.tensor_tensor(
+                out=h1, in0=shared("squashed", grp)[:, cols], in1=shared("gate%d" % GATE_O, grp)[:, cols], op=ALU.mult
+            )
+            nc.sync.dma_start(out=rows(out_0, part), in_=h1)
+
+        first, second, third = UNITS[:3]
+        widen_hh(first)
+        widen_hh(second)
+        turn_hh(first)
+        turn_hh(second)
+        widen_hh(third)
+        nc.vector.tensor_copy(
+            out=wz[:].bitcast(I32).rearrange("p (t m) -> p t m", t=4),
+            in_=wz_raw[:].bitcast(I32).rearrange("p (m t) -> p t m", t=4),
+        )
+        scale_hh(first)
+        nc.vector.tensor_copy(
+            out=wz_sc[:].rearrange("p (t m) -> p t m", t=4), in_=wz_raw_sc[:].rearrange("p (m t) -> p t m", t=4)
+        )
+        turn_h(first)
+        quantize("hh_t", hh_q, hh_qs, first)
+        scale_hh(second)
+        copy_h(first)
+        multiply_z(first, 0)
+        turn_h(second)
+        quantize("h_t", h_q, h_qs, first)
+        quantize("hh_t", hh_q, hh_qs, second)
+        bias_z(first, 0)
+        copy_h(second)
+        multiply_z(second, 0)
+        recurrent(0)
+        turn_hh(third)
+        quantize("h_t", h_q, h_qs, second)
+        quantize("z_t", z_q, z_qs, first)
+        bias_z(second, 0)
+        recurrent(1)
+        scale_hh(third)
+        quantize("z_t", z_q, z_qs, second)
+        modulate(0)
+        quantize("hh_t", hh_q, hh_qs, third)
+        turn_h(third)
+        copy_h(third)
+
+        last = len(chunks) - 1
+        done_at = {}
+        for n, (tile, g) in enumerate(chunks):
+            done_at[group_of[tile], g] = n
+        recurrent_next = 2
+        for n in range(len(chunks)):
+            q, s = divmod(n, 8)
+            ahead = UNITS[q + 2] if q + 2 < len(UNITS) else None
+            further = UNITS[q + 3] if q + 3 < len(UNITS) else None
+            if n + 1 <= last:
+                modulate(n + 1)
+            shift(n)
+            for step in range(2):
+                if recurrent_next <= min(last, n + R_AHEAD) and (step == 0 or n >= RAMP):
+                    recurrent(recurrent_next)
+                    recurrent_next += 1
+            for grp in GROUPS:
+                if done_at[grp, GATE_F] == n - 1:
+                    activate(grp, GATE_F, grp)
+                    forget(grp, nc.gpsimd)
+                if done_at[grp, GATE_I] == n - 1:
+                    activate(grp, GATE_I, grp)
+                if done_at[grp, GATE_G] == n - 1:
+                    activate(grp, GATE_G, grp)
+                    if grp != GROUPS[-1]:
+                        candidate(grp, grp, nc.gpsimd)
+                        cell(grp, grp, nc.gpsimd)
+                if done_at[grp, GATE_O] == n - 1:
+                    activate(grp, GATE_O, grp)
+            for grp in GROUPS:
+                if done_at[grp, GATE_G] + TANH_LAG == n:
+                    squash(grp, grp)
+                    if grp != GROUPS[1]:
+                        hidden(grp, grp, nc.gpsimd)
+            if ahead:
+                if s in (0, 1):
+                    multiply_z(ahead, s)
+                if s in (1, 2):
+                    bias_z(ahead, s - 1)
+                if n == 1:
+                    quantize("h_t", h_q, h_qs, ahead)
+                if s == 5:
+                    quantize("z_t", z_q, z_qs, ahead)
+            if further:
+                if s == 1:
+                    widen_hh(further)
+                if s == 2:
+                    turn_hh(further)
+                if s == 3:
+                    turn_h(further)
+                    copy_h(further)
+                if s == 4:
+                    scale_hh(further)
+                if s == 5:
+                    quantize("hh_t", hh_q, hh_qs, further)
+                    quantize("h_t", h_q, h_qs, further)
+            if n == done_at[GROUPS[2], GATE_G]:
+                hidden(GROUPS[1], GROUPS[1], nc.vector)
+
+        grp = GROUPS[-1]
+        parts = [(tile,) for tile in grp]
+        for part in parts:
+            candidate(grp, part, nc.vector)
+            activate(grp, GATE_O, part)
+        for part in parts:
+            cell(grp, part, nc.vector)
+            squash(grp, part)
+        for part in parts:
+            hidden(grp, part, nc.vector)

@@ -19,9 +19,10 @@ TILES = B // P
 PAIRS = TILES // 2
 GATE_I, GATE_G, GATE_F, GATE_O = range(4)
 GATE_ORDER = (GATE_F, GATE_I, GATE_G, GATE_O)
-R_AHEAD = 4
-RAMP = 4
-TANH_LAG = 5
+R_AHEAD = 5
+RAMP = 2
+TANH_LAG = 6
+SLOT = 5
 PAIRS_IN = ((0, 1), (2, 3), (4, 5), (6, 7))
 UNITS = ((0,), (1,), (2, 3), (4, 5), (6, 7))
 GROUPS = ((0, 1), (2, 3), (4, 5), (6, 7))
@@ -54,12 +55,17 @@ def tile_hyperlstmgeneratedscalebiasstep_w8_kernel(
                 u: keep.tile([P, len(u) * width], dtype, name="%s%d" % (name, u[0]), align_bytes=64) for u in UNITS
             }
 
-        hh_sb = {pair: keep.tile([P, 2 * K], U8, name="hh_sb%d" % pair[0]) for pair in PAIRS_IN}
+        hh_first = keep.tile([P, 2 * K], U8, name="hh_first")
+        hh_rest = keep.tile([P, (TILES - 2) * K], U8, name="hh_rest")
         h_sb = {pair: keep.tile([P, 2 * K], BF16, name="h_sb%d" % pair[0]) for pair in PAIRS_IN}
 
-        def loaded(tiles, u):
+        def loaded_h(u):
             j = u[0] % 2
-            return tiles[PAIRS_IN[u[0] // 2]][:, K * j : K * (j + len(u))]
+            return h_sb[PAIRS_IN[u[0] // 2]][:, K * j : K * (j + len(u))]
+
+        def loaded_hh(u):
+            src, j = (hh_first, u[0]) if u[0] < 2 else (hh_rest, u[0] - 2)
+            return src[:, K * j : K * (j + len(u))].bitcast(FP8)
 
         c_sb = {grp: keep.tile([P, len(grp) * H], BF16, name="c_sb%d" % grp[0]) for grp in GROUPS}
         hh_q, hh_qs = per_unit("hh_q", P, U32), per_unit("hh_qs", P, U8)
@@ -77,6 +83,7 @@ def tile_hyperlstmgeneratedscalebiasstep_w8_kernel(
         wd_sc = keep.tile([P, 2 * H], U8, name="wd_sc", align_bytes=64)
         hs = keep.tile([P, 4], F32, name="hs")
         bz_sb = keep.tile([P, 4], BF16, name="bz_sb")
+        hs_row = keep.tile([P, K], F32, name="hs_row")
         ident = keep.tile([P, P], F32, name="ident")
         warm = keep.tile([P, 1], F32, name="warm")
 
@@ -85,7 +92,6 @@ def tile_hyperlstmgeneratedscalebiasstep_w8_kernel(
         nc.vector.memset(wh_sc[:].bitcast(I32), 0)
         nc.vector.memset(wd_sc[:].bitcast(I32), 0)
         nc.scalar.activation(out=warm[:], in_=warm[:], func=ACT.Sigmoid)
-        nc.gpsimd.dma_start(out=hs[:], in_=hh_scale.rearrange("o (p t) -> p (o t)", t=4))
         nc.gpsimd.dma_start(out=bz_sb[:], in_=bz.rearrange("(p t) -> p t", t=4))
         make_identity(nc, ident[:])
 
@@ -108,68 +114,86 @@ def tile_hyperlstmgeneratedscalebiasstep_w8_kernel(
             both = words_of(wd_words).rearrange("p (a g n) -> p a g n", a=2, g=4)
             nc.sync.dma_start(out=wd[g][:].bitcast(I32), in_=both[:, :, g, :])
 
-        load_rows(hh_sb, hh_bytes, PAIRS_IN[0])
+        nc.sync.dma_start(out=hh_first[:], in_=rows(hh_bytes, PAIRS_IN[0]))
+        nc.sync.dma_start(out=hs[:], in_=hh_scale.rearrange("o (p t) -> p (o t)", t=4))
         nc.sync.dma_start(out=wz_raw[:].bitcast(I32), in_=words_of(wz_words))
         load_scales(wz_raw_sc, wz_scales, 1)
         load_rows(h_sb, h, PAIRS_IN[0])
-        load_rows(hh_sb, hh_bytes, PAIRS_IN[1])
+        nc.sync.dma_start(out=hh_rest[:], in_=rows(hh_bytes, range(2, TILES)))
+        load_rows(h_sb, h, PAIRS_IN[1])
         load_gate(GATE_ORDER[0])
         load_scales(wh_sc, wh_scales, 4)
         load_scales(wd_sc, wd_scales, 4)
-        load_rows(h_sb, h, PAIRS_IN[1])
         load_gate(GATE_ORDER[1])
-        load_rows(hh_sb, hh_bytes, PAIRS_IN[2])
         load_rows(c_sb, c, GROUPS[0])
         load_gate(GATE_ORDER[2])
-        load_gate(GATE_ORDER[3])
         load_rows(h_sb, h, PAIRS_IN[2])
-        load_rows(hh_sb, hh_bytes, PAIRS_IN[3])
+        load_gate(GATE_ORDER[3])
         load_rows(h_sb, h, PAIRS_IN[3])
         for grp in GROUPS[1:]:
             load_rows(c_sb, c, grp)
 
         staged = {}
 
-        def widen_hh(u):
-            wide = work.tile([P, len(u) * K], BF16, name="hh_wide")
-            nc.scalar.copy(out=wide[:], in_=loaded(hh_sb, u).bitcast(FP8))
-            staged["wide", u] = wide
+        def spread(column_tile, row_tile):
+            src = bank("prep")
+            for t in range(4):
+                nc.tensor.transpose(
+                    src[:, P * t : P * (t + 1)], column_tile[:, t : t + 1].to_broadcast([P, P]), ident[:]
+                )
+            nc.scalar.copy(
+                out=row_tile[:].rearrange("p (n t) -> p n t", t=4), in_=src[:].rearrange("p (t n) -> p n t", t=4)
+            )
 
-        def turn(src, u):
-            words = src.bitcast(F32)
-            dst = bank("prep")
+        def over_tiles(row_tile, u):
+            return row_tile[:].unsqueeze(1).to_broadcast([P, len(u), K])
+
+        def widen_hh(u, copy):
+            wide = work.tile([P, len(u) * K], BF16, name="hh_wide", bufs=3)
+            copy(out=wide[:], in_=loaded_hh(u))
+            staged["hh_wide", u] = wide[:]
+
+        def scale_rows(u, eng, src):
+            dst = work.tile([P, len(u) * K], BF16, name="hh_rows")
+            eng.tensor_tensor(
+                out=dst[:].rearrange("p (j k) -> p j k", k=K),
+                in0=src.rearrange("p (j k) -> p j k", k=K),
+                in1=over_tiles(hs_row, u),
+                op=ALU.mult,
+            )
+            staged["hh_rows", u] = dst[:]
+
+        def turn(name, u, role="prep"):
+            words = staged[name, u].bitcast(F32)
+            dst = bank(role)
             for half in range(2):
                 for j in range(len(u)):
                     col = P * (len(u) * half + j)
                     nc.tensor.transpose(dst[:, col : col + P], words[:, 256 * j + half : 256 * (j + 1) : 2], ident[:])
             return dst[:, : 2 * P * len(u)]
 
-        def turn_hh(u):
-            staged["hh_bank", u] = turn(staged["wide", u][:], u)
+        def copy_turned(name, u, src):
+            dst = work.tile([P, len(u) * K], BF16, name=name + "_t", align_bytes=64, bufs=3)
+            nc.scalar.copy(
+                out=dst[:].bitcast(F32).rearrange("p (n a) -> p n a", a=2), in_=src.rearrange("p (a n) -> p n a", a=2)
+            )
+            staged[name + "_t", u] = dst
 
-        def turn_h(u):
-            staged["h_bank", u] = turn(loaded(h_sb, u), u)
-
-        def scale_hh(u):
-            dst = work.tile([P, len(u) * K], BF16, name="hh_t", align_bytes=64)
+        def scale_turned(u, src):
+            dst = work.tile([P, len(u) * K], BF16, name="hh_t", align_bytes=64, bufs=3)
             nc.vector.tensor_tensor(
                 out=dst[:].rearrange("p (n a e) -> p n a e", a=2, e=2),
-                in0=staged["hh_bank", u].bitcast(BF16).rearrange("p (a n e) -> p n a e", a=2, e=2),
+                in0=src.bitcast(BF16).rearrange("p (a n e) -> p n a e", a=2, e=2),
                 in1=hs[:].rearrange("p (a e) -> p a e", a=2).unsqueeze(1).to_broadcast([P, len(u) * P, 2, 2]),
                 op=ALU.mult,
             )
             staged["hh_t", u] = dst
 
-        def copy_h(u):
-            dst = work.tile([P, len(u) * K], BF16, name="h_t", align_bytes=64)
-            nc.scalar.copy(
-                out=dst[:].bitcast(F32).rearrange("p (n a) -> p n a", a=2),
-                in_=staged["h_bank", u].rearrange("p (a n) -> p n a", a=2),
-            )
-            staged["h_t", u] = dst
+        codes_of = {"hh": (hh_q, hh_qs), "h": (h_q, h_qs), "z": (z_q, z_qs)}
 
-        def quantize(name, codes, scales, u):
-            nc.vector.quantize_mx(out=codes[u][:].bitcast(FP8X4), scales=scales[u][:], in_=staged[name, u][:])
+        def quantize(name, u):
+            codes, scales = codes_of[name]
+            nc.vector.quantize_mx(out=codes[u][:].bitcast(FP8X4), scales=scales[u][:], in_=staged[name + "_t", u][:])
 
         def multiply_z(u, j):
             dst = bank("prep")
@@ -196,6 +220,9 @@ def tile_hyperlstmgeneratedscalebiasstep_w8_kernel(
                 in1=bz_sb[:].unsqueeze(1).to_broadcast([P, P, 4]),
                 op=ALU.add,
             )
+
+        for u in UNITS:
+            staged["h_rows", u] = loaded_h(u)
 
         chunks = [(tile, g) for grp in GROUPS for g in GATE_ORDER for tile in grp]
 
@@ -240,9 +267,15 @@ def tile_hyperlstmgeneratedscalebiasstep_w8_kernel(
                 out=pre_slice(n), in0=d[:], scalar=1.0, in1=staged["r", n][:], op0=ALU.add, op1=ALU.mult
             )
 
+        def multiply_beta(n):
+            tile, g = chunks[n]
+            staged["beta", n] = gate_matmul(
+                "beta_bank", z_q, z_qs, tile, wd[g][:, 1, :], wd_scales_of(4 * H + H * g)
+            )
+
         def shift(n):
             tile, g = chunks[n]
-            beta = gate_matmul("beta_bank", z_q, z_qs, tile, wd[g][:, 1, :], wd_scales_of(4 * H + H * g))
+            beta = staged["beta", n]
             if g == GATE_F:
                 nc.vector.scalar_tensor_tensor(
                     out=pre_slice(n), in0=beta[:], scalar=1.0, in1=pre_slice(n), op0=ALU.add, op1=ALU.add
@@ -296,60 +329,61 @@ def tile_hyperlstmgeneratedscalebiasstep_w8_kernel(
             )
             nc.sync.dma_start(out=rows(out_0, part), in_=h1)
 
-        first, second, third = UNITS[:3]
-        widen_hh(first)
-        widen_hh(second)
-        turn_hh(first)
-        turn_hh(second)
-        widen_hh(third)
+        first, second, third, fourth, fifth = UNITS
+        widen_hh(first, nc.vector.tensor_copy)
+        widen_hh(second, nc.scalar.copy)
+        hh_bank = [turn("hh_wide", u, "d_bank") for u in (first, second)]
         nc.vector.tensor_copy(
             out=wz[:].bitcast(I32).rearrange("p (t m) -> p t m", t=4),
             in_=wz_raw[:].bitcast(I32).rearrange("p (m t) -> p t m", t=4),
         )
-        scale_hh(first)
+        scale_turned(first, hh_bank[0])
         nc.vector.tensor_copy(
             out=wz_sc[:].rearrange("p (t m) -> p t m", t=4), in_=wz_raw_sc[:].rearrange("p (m t) -> p t m", t=4)
         )
-        turn_h(first)
-        quantize("hh_t", hh_q, hh_qs, first)
-        scale_hh(second)
-        copy_h(first)
+        copy_turned("h", first, turn("h_rows", first, "beta_bank"))
+        widen_hh(third, nc.scalar.copy)
+        quantize("hh", first)
+        scale_turned(second, hh_bank[1])
         multiply_z(first, 0)
-        turn_h(second)
-        quantize("h_t", h_q, h_qs, first)
-        quantize("hh_t", hh_q, hh_qs, second)
+        copy_turned("h", second, turn("h_rows", second, "beta_bank"))
+        quantize("hh", second)
         bias_z(first, 0)
-        copy_h(second)
         multiply_z(second, 0)
-        recurrent(0)
-        turn_hh(third)
-        quantize("h_t", h_q, h_qs, second)
-        quantize("z_t", z_q, z_qs, first)
+        third_bank = turn("hh_wide", third, "d_bank")
+        widen_hh(fourth, nc.scalar.copy)
+        copy_turned("h", third, turn("h_rows", third, "beta_bank"))
+        quantize("h", first)
         bias_z(second, 0)
+        quantize("z", first)
+        quantize("h", second)
+        recurrent(0)
         recurrent(1)
-        scale_hh(third)
-        quantize("z_t", z_q, z_qs, second)
+        quantize("z", second)
+        scale_turned(third, third_bank)
+        quantize("h", third)
+        quantize("hh", third)
         modulate(0)
-        quantize("hh_t", hh_q, hh_qs, third)
-        turn_h(third)
-        copy_h(third)
+        modulate(1)
+        recurrent(2)
+        spread(hs, hs_row)
+        scale_rows(fourth, nc.gpsimd, staged["hh_wide", fourth])
 
         last = len(chunks) - 1
         done_at = {}
         for n, (tile, g) in enumerate(chunks):
             done_at[group_of[tile], g] = n
-        recurrent_next = 2
+        final = GROUPS[-1]
+        parts = [(tile,) for tile in final]
+        recurrent_next = 3
         for n in range(len(chunks)):
             q, s = divmod(n, 8)
             ahead = UNITS[q + 2] if q + 2 < len(UNITS) else None
             further = UNITS[q + 3] if q + 3 < len(UNITS) else None
-            if n + 1 <= last:
-                modulate(n + 1)
+            multiply_beta(n)
+            if n + 2 <= last:
+                modulate(n + 2)
             shift(n)
-            for step in range(2):
-                if recurrent_next <= min(last, n + R_AHEAD) and (step == 0 or n >= RAMP):
-                    recurrent(recurrent_next)
-                    recurrent_next += 1
             for grp in GROUPS:
                 if done_at[grp, GATE_F] == n - 1:
                     activate(grp, GATE_F, grp)
@@ -358,48 +392,44 @@ def tile_hyperlstmgeneratedscalebiasstep_w8_kernel(
                     activate(grp, GATE_I, grp)
                 if done_at[grp, GATE_G] == n - 1:
                     activate(grp, GATE_G, grp)
-                    if grp != GROUPS[-1]:
+                    if grp != final:
                         candidate(grp, grp, nc.gpsimd)
                         cell(grp, grp, nc.gpsimd)
                 if done_at[grp, GATE_O] == n - 1:
                     activate(grp, GATE_O, grp)
-            for grp in GROUPS:
+            for step in range(2):
+                if recurrent_next <= min(last, n + R_AHEAD) and (step == 0 or n >= RAMP):
+                    recurrent(recurrent_next)
+                    recurrent_next += 1
+            if n == 1:
+                widen_hh(fifth, nc.scalar.copy)
+                scale_rows(fifth, nc.gpsimd, staged["hh_wide", fifth])
+            for grp in GROUPS[:-1]:
                 if done_at[grp, GATE_G] + TANH_LAG == n:
                     squash(grp, grp)
-                    if grp != GROUPS[1]:
-                        hidden(grp, grp, nc.gpsimd)
+                    hidden(grp, grp, nc.gpsimd)
             if ahead:
                 if s in (0, 1):
                     multiply_z(ahead, s)
                 if s in (1, 2):
                     bias_z(ahead, s - 1)
-                if n == 1:
-                    quantize("h_t", h_q, h_qs, ahead)
-                if s == 5:
-                    quantize("z_t", z_q, z_qs, ahead)
             if further:
-                if s == 1:
-                    widen_hh(further)
                 if s == 2:
-                    turn_hh(further)
-                if s == 3:
-                    turn_h(further)
-                    copy_h(further)
+                    copy_turned("h", further, turn("h_rows", further))
                 if s == 4:
-                    scale_hh(further)
-                if s == 5:
-                    quantize("hh_t", hh_q, hh_qs, further)
-                    quantize("h_t", h_q, h_qs, further)
-            if n == done_at[GROUPS[2], GATE_G]:
-                hidden(GROUPS[1], GROUPS[1], nc.vector)
+                    copy_turned("hh", further, turn("hh_rows", further))
+            if s == SLOT:
+                if ahead:
+                    quantize("z", ahead)
+                if further:
+                    quantize("h", further)
+                    quantize("hh", further)
 
-        grp = GROUPS[-1]
-        parts = [(tile,) for tile in grp]
         for part in parts:
-            candidate(grp, part, nc.vector)
-            activate(grp, GATE_O, part)
+            activate(final, GATE_O, part)
+            candidate(final, part, nc.vector)
         for part in parts:
-            cell(grp, part, nc.vector)
-            squash(grp, part)
+            cell(final, part, nc.vector)
+            squash(final, part)
         for part in parts:
-            hidden(grp, part, nc.vector)
+            hidden(final, part, nc.vector)

@@ -20,11 +20,21 @@ PAIRS = TILES // 2
 GATE_I, GATE_G, GATE_F, GATE_O = range(4)
 GATE_ORDER = (GATE_F, GATE_I, GATE_G, GATE_O)
 R_AHEAD = 5
-RAMP = 2
+RAMP = 4
+THF = 4
+WF = 0
+SLOTS = (5, 13)
 TANH_LAG = 6
 SLOT = 5
 PAIRS_IN = ((0, 1), (2, 3), (4, 5), (6, 7))
 UNITS = ((0,), (1,), (2, 3), (4, 5), (6, 7))
+FIRST, SECOND, THIRD, FOURTH, FIFTH = UNITS
+BATCHES = tuple(((name, u),) for name in ("hh", "h", "z") for u in (FIRST, SECOND)) + (
+    (("h", THIRD), ("hh", THIRD)),
+    (("z", THIRD), ("h", FOURTH), ("hh", FOURTH), ("hh", FIFTH)),
+    (("h", FIFTH),),
+    (("z", FOURTH), ("z", FIFTH)),
+)
 GROUPS = ((0, 1), (2, 3), (4, 5), (6, 7))
 
 FLOPS = 2 * B * K * (K + 8 * H + 4 * H)
@@ -50,11 +60,6 @@ def tile_hyperlstmgeneratedscalebiasstep_w8_kernel(
         def bank(role):
             return psum.tile([P, 512], F32, name=role)
 
-        def per_unit(name, width, dtype):
-            return {
-                u: keep.tile([P, len(u) * width], dtype, name="%s%d" % (name, u[0]), align_bytes=64) for u in UNITS
-            }
-
         hh_first = keep.tile([P, 2 * K], U8, name="hh_first")
         hh_rest = keep.tile([P, (TILES - 2) * K], U8, name="hh_rest")
         h_sb = {pair: keep.tile([P, 2 * K], BF16, name="h_sb%d" % pair[0]) for pair in PAIRS_IN}
@@ -68,10 +73,20 @@ def tile_hyperlstmgeneratedscalebiasstep_w8_kernel(
             return src[:, K * j : K * (j + len(u))].bitcast(FP8)
 
         c_sb = {grp: keep.tile([P, len(grp) * H], BF16, name="c_sb%d" % grp[0]) for grp in GROUPS}
-        hh_q, hh_qs = per_unit("hh_q", P, U32), per_unit("hh_qs", P, U8)
-        h_q, h_qs = per_unit("h_q", P, U32), per_unit("h_qs", P, U8)
-        z_q, z_qs = per_unit("z_q", P, U32), per_unit("z_qs", P, U8)
-        unit_of = {tile: u for u in UNITS for tile in u}
+        staging, codes_of, scales_of, batch_tiles = {}, {}, {}, {}
+        for b, batch in enumerate(BATCHES):
+            tiles_in = sum(len(u) for name, u in batch)
+            values = keep.tile([P, tiles_in * K], BF16, name="values%d" % b, align_bytes=64)
+            codes = keep.tile([P, tiles_in * P], U32, name="codes%d" % b, align_bytes=64)
+            scales = keep.tile([P, tiles_in * P], U8, name="scales%d" % b, align_bytes=64)
+            batch_tiles[batch] = (values, codes, scales)
+            at = 0
+            for name, u in batch:
+                staging[name, u] = values[:, K * at : K * (at + len(u))]
+                for tile in u:
+                    codes_of[name, tile] = codes[:, P * at : P * (at + 1)].bitcast(FP8X4)
+                    scales_of[name, tile] = scales[:, P * at : P * (at + 1)]
+                    at += 1
         group_of = {tile: grp for grp in GROUPS for tile in grp}
         wz_raw = keep.tile([P, K], U32, name="wz_raw")
         wz_raw_sc = keep.tile([P, K], U8, name="wz_raw_sc")
@@ -84,16 +99,17 @@ def tile_hyperlstmgeneratedscalebiasstep_w8_kernel(
         hs = keep.tile([P, 4], F32, name="hs")
         bz_sb = keep.tile([P, 4], BF16, name="bz_sb")
         hs_row = keep.tile([P, K], F32, name="hs_row")
-        ident = keep.tile([P, P], F32, name="ident")
         warm = keep.tile([P, 1], F32, name="warm")
+        ident = keep.tile([P, P], F32, name="ident")
 
         nc.vector.memset(warm[:], 0.0)
+        nc.scalar.activation(out=warm[:], in_=warm[:], func=ACT.Sigmoid)
         nc.vector.memset(wz_raw_sc[:].bitcast(I32), 0)
         nc.vector.memset(wh_sc[:].bitcast(I32), 0)
         nc.vector.memset(wd_sc[:].bitcast(I32), 0)
-        nc.scalar.activation(out=warm[:], in_=warm[:], func=ACT.Sigmoid)
+        nc.vector.memset(ident[:], 0.0)
         nc.gpsimd.dma_start(out=bz_sb[:], in_=bz.rearrange("(p t) -> p t", t=4))
-        make_identity(nc, ident[:])
+        make_identity(nc, ident[:], nomemset=True)
 
         def rows(x, tiles):
             return rows_of(x)[:, tiles[0] : tiles[-1] + 1, :].rearrange("p t n -> p (t n)")
@@ -120,10 +136,10 @@ def tile_hyperlstmgeneratedscalebiasstep_w8_kernel(
         load_scales(wz_raw_sc, wz_scales, 1)
         load_rows(h_sb, h, PAIRS_IN[0])
         nc.sync.dma_start(out=hh_rest[:], in_=rows(hh_bytes, range(2, TILES)))
-        load_rows(h_sb, h, PAIRS_IN[1])
-        load_gate(GATE_ORDER[0])
         load_scales(wh_sc, wh_scales, 4)
         load_scales(wd_sc, wd_scales, 4)
+        load_rows(h_sb, h, PAIRS_IN[1])
+        load_gate(GATE_ORDER[0])
         load_gate(GATE_ORDER[1])
         load_rows(c_sb, c, GROUPS[0])
         load_gate(GATE_ORDER[2])
@@ -173,49 +189,41 @@ def tile_hyperlstmgeneratedscalebiasstep_w8_kernel(
             return dst[:, : 2 * P * len(u)]
 
         def copy_turned(name, u, src):
-            dst = work.tile([P, len(u) * K], BF16, name=name + "_t", align_bytes=64, bufs=3)
             nc.scalar.copy(
-                out=dst[:].bitcast(F32).rearrange("p (n a) -> p n a", a=2), in_=src.rearrange("p (a n) -> p n a", a=2)
+                out=staging[name, u].bitcast(F32).rearrange("p (n a) -> p n a", a=2),
+                in_=src.rearrange("p (a n) -> p n a", a=2),
             )
-            staged[name + "_t", u] = dst
 
         def scale_turned(u, src):
-            dst = work.tile([P, len(u) * K], BF16, name="hh_t", align_bytes=64, bufs=3)
             nc.vector.tensor_tensor(
-                out=dst[:].rearrange("p (n a e) -> p n a e", a=2, e=2),
+                out=staging["hh", u].rearrange("p (n a e) -> p n a e", a=2, e=2),
                 in0=src.bitcast(BF16).rearrange("p (a n e) -> p n a e", a=2, e=2),
                 in1=hs[:].rearrange("p (a e) -> p a e", a=2).unsqueeze(1).to_broadcast([P, len(u) * P, 2, 2]),
                 op=ALU.mult,
             )
-            staged["hh_t", u] = dst
 
-        codes_of = {"hh": (hh_q, hh_qs), "h": (h_q, h_qs), "z": (z_q, z_qs)}
-
-        def quantize(name, u):
-            codes, scales = codes_of[name]
-            nc.vector.quantize_mx(out=codes[u][:].bitcast(FP8X4), scales=scales[u][:], in_=staged[name + "_t", u][:])
+        def quantize(*batch):
+            values, codes, scales = batch_tiles[batch]
+            nc.vector.quantize_mx(out=codes[:].bitcast(FP8X4), scales=scales[:], in_=values[:])
 
         def multiply_z(u, j):
             dst = bank("prep")
-            cols = slice(P * j, P * (j + 1))
             for t in range(4):
                 chans = slice(P * t, P * (t + 1))
                 nc.tensor.matmul_mx(
                     out=dst[:, chans],
                     lhsT=wz[:, chans].bitcast(FP8X4),
                     lhsT_scale=wz_sc[:, chans],
-                    rhs=hh_q[u][:, cols].bitcast(FP8X4),
-                    rhs_scale=hh_qs[u][:, cols],
+                    rhs=codes_of["hh", u[j]],
+                    rhs_scale=scales_of["hh", u[j]],
                     start=True,
                     stop=True,
                 )
             staged["z_bank", u, j] = dst
 
         def bias_z(u, j):
-            if j == 0:
-                staged["z_t", u] = work.tile([P, len(u) * K], BF16, name="z_t", align_bytes=64)
             nc.vector.tensor_tensor(
-                out=staged["z_t", u][:, K * j : K * (j + 1)].rearrange("p (n t) -> p n t", t=4),
+                out=staging["z", u][:, K * j : K * (j + 1)].rearrange("p (n t) -> p n t", t=4),
                 in0=staged["z_bank", u, j][:].rearrange("p (t n) -> p n t", t=4),
                 in1=bz_sb[:].unsqueeze(1).to_broadcast([P, P, 4]),
                 op=ALU.add,
@@ -226,14 +234,12 @@ def tile_hyperlstmgeneratedscalebiasstep_w8_kernel(
 
         chunks = [(tile, g) for grp in GROUPS for g in GATE_ORDER for tile in grp]
 
-        def gate_matmul(role, codes, scales, tile, weights, weight_scales):
-            u = unit_of[tile]
-            cols = slice(P * (tile - u[0]), P * (tile - u[0] + 1))
+        def gate_matmul(role, name, tile, weights, weight_scales):
             dst = bank(role)
             nc.tensor.matmul_mx(
                 out=dst[:],
-                lhsT=codes[u][:, cols].bitcast(FP8X4),
-                lhsT_scale=scales[u][:, cols],
+                lhsT=codes_of[name, tile],
+                lhsT_scale=scales_of[name, tile],
                 rhs=weights.bitcast(FP8X4),
                 rhs_scale=weight_scales,
                 start=True,
@@ -247,7 +253,7 @@ def tile_hyperlstmgeneratedscalebiasstep_w8_kernel(
 
         def recurrent(n):
             tile, g = chunks[n]
-            src = gate_matmul("r_bank", h_q, h_qs, tile, wh[g][:], wh_sc[4 * g :, :])
+            src = gate_matmul("r_bank", "h", tile, wh[g][:], wh_sc[4 * g :, :])
             r = work.tile([P, H], F32, name="r", bufs=R_AHEAD + 2)
             nc.scalar.copy(out=r[:], in_=src[:])
             staged["r", n] = r
@@ -260,9 +266,12 @@ def tile_hyperlstmgeneratedscalebiasstep_w8_kernel(
             j = tile - grp[0]
             return staged["pre", grp, g][:, H * j : H * (j + 1)]
 
-        def modulate(n):
+        def multiply_d(n):
             tile, g = chunks[n]
-            d = gate_matmul("d_bank", z_q, z_qs, tile, wd[g][:, 0, :], wd_scales_of(H * g))
+            staged["d", n] = gate_matmul("d_bank", "z", tile, wd[g][:, 0, :], wd_scales_of(H * g))
+
+        def modulate(n):
+            d = staged["d", n]
             nc.vector.scalar_tensor_tensor(
                 out=pre_slice(n), in0=d[:], scalar=1.0, in1=staged["r", n][:], op0=ALU.add, op1=ALU.mult
             )
@@ -270,7 +279,7 @@ def tile_hyperlstmgeneratedscalebiasstep_w8_kernel(
         def multiply_beta(n):
             tile, g = chunks[n]
             staged["beta", n] = gate_matmul(
-                "beta_bank", z_q, z_qs, tile, wd[g][:, 1, :], wd_scales_of(4 * H + H * g)
+                "beta_bank", "z", tile, wd[g][:, 1, :], wd_scales_of(4 * H + H * g)
             )
 
         def shift(n):
@@ -343,27 +352,28 @@ def tile_hyperlstmgeneratedscalebiasstep_w8_kernel(
         )
         copy_turned("h", first, turn("h_rows", first, "beta_bank"))
         widen_hh(third, nc.scalar.copy)
-        quantize("hh", first)
+        quantize(("hh", first))
         scale_turned(second, hh_bank[1])
         multiply_z(first, 0)
         copy_turned("h", second, turn("h_rows", second, "beta_bank"))
-        quantize("hh", second)
+        quantize(("hh", second))
         bias_z(first, 0)
         multiply_z(second, 0)
         third_bank = turn("hh_wide", third, "d_bank")
         widen_hh(fourth, nc.scalar.copy)
         copy_turned("h", third, turn("h_rows", third, "beta_bank"))
-        quantize("h", first)
+        quantize(("h", first))
         bias_z(second, 0)
-        quantize("z", first)
-        quantize("h", second)
+        quantize(("z", first))
+        quantize(("h", second))
         recurrent(0)
         recurrent(1)
-        quantize("z", second)
+        quantize(("z", second))
         scale_turned(third, third_bank)
-        quantize("h", third)
-        quantize("hh", third)
+        multiply_d(0)
         modulate(0)
+        quantize(*BATCHES[-4])
+        multiply_d(1)
         modulate(1)
         recurrent(2)
         spread(hs, hs_row)
@@ -377,13 +387,15 @@ def tile_hyperlstmgeneratedscalebiasstep_w8_kernel(
         parts = [(tile,) for tile in final]
         recurrent_next = 3
         for n in range(len(chunks)):
-            q, s = divmod(n, 8)
-            ahead = UNITS[q + 2] if q + 2 < len(UNITS) else None
-            further = UNITS[q + 3] if q + 3 < len(UNITS) else None
-            multiply_beta(n)
+            if n - 1 in SLOTS:
+                multiply_beta(n)
+                shift(n)
             if n + 2 <= last:
+                multiply_d(n + 2)
                 modulate(n + 2)
-            shift(n)
+            if n - 1 not in SLOTS:
+                multiply_beta(n)
+                shift(n)
             for grp in GROUPS:
                 if done_at[grp, GATE_F] == n - 1:
                     activate(grp, GATE_F, grp)
@@ -401,30 +413,35 @@ def tile_hyperlstmgeneratedscalebiasstep_w8_kernel(
                 if recurrent_next <= min(last, n + R_AHEAD) and (step == 0 or n >= RAMP):
                     recurrent(recurrent_next)
                     recurrent_next += 1
-            if n == 1:
+            if n == WF:
                 widen_hh(fifth, nc.scalar.copy)
                 scale_rows(fifth, nc.gpsimd, staged["hh_wide", fifth])
-            for grp in GROUPS[:-1]:
+            for grp in GROUPS[:2]:
                 if done_at[grp, GATE_G] + TANH_LAG == n:
                     squash(grp, grp)
                     hidden(grp, grp, nc.gpsimd)
-            if ahead:
-                if s in (0, 1):
-                    multiply_z(ahead, s)
-                if s in (1, 2):
-                    bias_z(ahead, s - 1)
-            if further:
-                if s == 2:
-                    copy_turned("h", further, turn("h_rows", further))
-                if s == 4:
-                    copy_turned("hh", further, turn("hh_rows", further))
-            if s == SLOT:
-                if ahead:
-                    quantize("z", ahead)
-                if further:
-                    quantize("h", further)
-                    quantize("hh", further)
+            if n == last - 2:
+                squash(GROUPS[2], GROUPS[2])
+            for u, start in ((third, 0), (fourth, 8), (fifth, 10)):
+                if n - start in (0, 1):
+                    multiply_z(u, n - start)
+                if n - start in (1, 2):
+                    bias_z(u, n - start - 1)
+            if n == 2:
+                copy_turned("h", fourth, turn("h_rows", fourth))
+            if n == 3:
+                copy_turned("hh", fourth, turn("hh_rows", fourth))
+            if n == 4:
+                copy_turned("hh", fifth, turn("hh_rows", fifth))
+            if n == 5:
+                quantize(*BATCHES[-2])
+                quantize(*BATCHES[-3])
+            if n == THF:
+                copy_turned("h", fifth, turn("h_rows", fifth))
+            if n == 13:
+                quantize(*BATCHES[-1])
 
+        hidden(GROUPS[2], GROUPS[2], nc.vector)
         for part in parts:
             activate(final, GATE_O, part)
             candidate(final, part, nc.vector)

@@ -20,10 +20,10 @@ PAIRS = TILES // 2
 GATE_I, GATE_G, GATE_F, GATE_O = range(4)
 GATE_ORDER = (GATE_F, GATE_I, GATE_G, GATE_O)
 R_AHEAD = 5
-RAMP = 4
+RAMP = 6
 THF = 4
 WF = 0
-SLOTS = (5, 13)
+SLOTS = (13,)
 TANH_LAG = 6
 SLOT = 5
 PAIRS_IN = ((0, 1), (2, 3), (4, 5), (6, 7))
@@ -31,8 +31,8 @@ UNITS = ((0,), (1,), (2, 3), (4, 5), (6, 7))
 FIRST, SECOND, THIRD, FOURTH, FIFTH = UNITS
 BATCHES = tuple(((name, u),) for name in ("hh", "h", "z") for u in (FIRST, SECOND)) + (
     (("h", THIRD), ("hh", THIRD)),
-    (("z", THIRD), ("h", FOURTH), ("hh", FOURTH), ("hh", FIFTH)),
-    (("h", FIFTH),),
+    (("z", THIRD),),
+    (("h", FOURTH), ("hh", FOURTH), ("hh", FIFTH), ("h", FIFTH)),
     (("z", FOURTH), ("z", FIFTH)),
 )
 GROUPS = ((0, 1), (2, 3), (4, 5), (6, 7))
@@ -100,11 +100,13 @@ def tile_hyperlstmgeneratedscalebiasstep_w8_kernel(
         bz_sb = keep.tile([P, 4], BF16, name="bz_sb")
         hs_row = keep.tile([P, K], F32, name="hs_row")
         warm = keep.tile([P, 1], F32, name="warm")
+        idle = keep.tile([P, H], BF16, name="idle")
         ident = keep.tile([P, P], F32, name="ident")
 
         nc.vector.memset(warm[:], 0.0)
         nc.scalar.activation(out=warm[:], in_=warm[:], func=ACT.Sigmoid)
         nc.vector.memset(wz_raw_sc[:].bitcast(I32), 0)
+        nc.vector.memset(idle[:].bitcast(I32), 0)
         nc.vector.memset(wh_sc[:].bitcast(I32), 0)
         nc.vector.memset(wd_sc[:].bitcast(I32), 0)
         nc.vector.memset(ident[:], 0.0)
@@ -141,15 +143,20 @@ def tile_hyperlstmgeneratedscalebiasstep_w8_kernel(
         load_rows(h_sb, h, PAIRS_IN[1])
         load_gate(GATE_ORDER[0])
         load_gate(GATE_ORDER[1])
-        load_rows(c_sb, c, GROUPS[0])
-        load_gate(GATE_ORDER[2])
         load_rows(h_sb, h, PAIRS_IN[2])
-        load_gate(GATE_ORDER[3])
+        load_gate(GATE_ORDER[2])
+        load_rows(c_sb, c, GROUPS[0])
         load_rows(h_sb, h, PAIRS_IN[3])
+        load_gate(GATE_ORDER[3])
         for grp in GROUPS[1:]:
             load_rows(c_sb, c, grp)
 
         staged = {}
+
+        def keep_clock(count):
+            unread = bank("r_bank")
+            for rep in range(count):
+                nc.tensor.matmul(unread[:], lhsT=idle[:, :P], rhs=idle[:], start=True, stop=True)
 
         def spread(column_tile, row_tile):
             src = bank("prep")
@@ -251,10 +258,10 @@ def tile_hyperlstmgeneratedscalebiasstep_w8_kernel(
             plane, col = divmod(first_col, 2 * H)
             return wd_sc[4 * plane :, col : col + H]
 
-        def recurrent(n):
+        def recurrent(n, role="r_bank"):
             tile, g = chunks[n]
-            src = gate_matmul("r_bank", "h", tile, wh[g][:], wh_sc[4 * g :, :])
-            r = work.tile([P, H], F32, name="r", bufs=R_AHEAD + 2)
+            src = gate_matmul(role, "h", tile, wh[g][:], wh_sc[4 * g :, :])
+            r = work.tile([P, H], F32, name="r", bufs=R_AHEAD + 4)
             nc.scalar.copy(out=r[:], in_=src[:])
             staged["r", n] = r
 
@@ -339,6 +346,7 @@ def tile_hyperlstmgeneratedscalebiasstep_w8_kernel(
             nc.sync.dma_start(out=rows(out_0, part), in_=h1)
 
         first, second, third, fourth, fifth = UNITS
+        keep_clock(4)
         widen_hh(first, nc.vector.tensor_copy)
         widen_hh(second, nc.scalar.copy)
         hh_bank = [turn("hh_wide", u, "d_bank") for u in (first, second)]
@@ -351,14 +359,17 @@ def tile_hyperlstmgeneratedscalebiasstep_w8_kernel(
             out=wz_sc[:].rearrange("p (t m) -> p t m", t=4), in_=wz_raw_sc[:].rearrange("p (m t) -> p t m", t=4)
         )
         copy_turned("h", first, turn("h_rows", first, "beta_bank"))
+        keep_clock(2)
         widen_hh(third, nc.scalar.copy)
         quantize(("hh", first))
         scale_turned(second, hh_bank[1])
         multiply_z(first, 0)
+        keep_clock(1)
         copy_turned("h", second, turn("h_rows", second, "beta_bank"))
         quantize(("hh", second))
         bias_z(first, 0)
         multiply_z(second, 0)
+        keep_clock(1)
         third_bank = turn("hh_wide", third, "d_bank")
         widen_hh(fourth, nc.scalar.copy)
         copy_turned("h", third, turn("h_rows", third, "beta_bank"))
@@ -410,8 +421,8 @@ def tile_hyperlstmgeneratedscalebiasstep_w8_kernel(
                 if done_at[grp, GATE_O] == n - 1:
                     activate(grp, GATE_O, grp)
             for step in range(2):
-                if recurrent_next <= min(last, n + R_AHEAD) and (step == 0 or n >= RAMP):
-                    recurrent(recurrent_next)
+                if recurrent_next <= min(last, n + R_AHEAD + (2 if n >= 12 else 0)) and (step == 0 or n >= RAMP):
+                    recurrent(recurrent_next, "prep" if n >= 12 and recurrent_next % 2 else "r_bank")
                     recurrent_next += 1
             if n == WF:
                 widen_hh(fifth, nc.scalar.copy)
@@ -422,7 +433,7 @@ def tile_hyperlstmgeneratedscalebiasstep_w8_kernel(
                     hidden(grp, grp, nc.gpsimd)
             if n == last - 2:
                 squash(GROUPS[2], GROUPS[2])
-            for u, start in ((third, 0), (fourth, 8), (fifth, 10)):
+            for u, start in ((third, 0), (fourth, 7), (fifth, 9)):
                 if n - start in (0, 1):
                     multiply_z(u, n - start)
                 if n - start in (1, 2):
@@ -434,8 +445,8 @@ def tile_hyperlstmgeneratedscalebiasstep_w8_kernel(
             if n == 4:
                 copy_turned("hh", fifth, turn("hh_rows", fifth))
             if n == 5:
-                quantize(*BATCHES[-2])
                 quantize(*BATCHES[-3])
+                quantize(*BATCHES[-2])
             if n == THF:
                 copy_turned("h", fifth, turn("h_rows", fifth))
             if n == 13:

from contextlib import ExitStack

import concourse.mybir as mybir
from concourse.masks import make_identity

F32 = mybir.dt.float32
BF16 = mybir.dt.bfloat16
I32 = mybir.dt.int32
U32 = mybir.dt.uint32
U8 = mybir.dt.uint8
FP8 = mybir.dt.float8_e4m3fn
FP8X4 = mybir.dt.float8_e4m3fn_x4
ALU = mybir.AluOpType
ACT = mybir.ActivationFunctionType

B, K, H = 1024, 512, 512
P = 128
TILES = B // P
PAIRS = TILES // 2
GATE_I, GATE_G, GATE_F, GATE_O = range(4)
GATE_ORDER = (GATE_F, GATE_I, GATE_G, GATE_O)
R_AHEAD = 5
RAMP = 6
THF = 4
WF = 0
SLOTS = (13,)
TANH_LAG = 6
SLOT = 5
PAIRS_IN = ((0, 1), (2, 3), (4, 5), (6, 7))
UNITS = ((0,), (1,), (2, 3), (4, 5), (6, 7))
FIRST, SECOND, THIRD, FOURTH, FIFTH = UNITS
BATCHES = tuple(((name, u),) for name in ("hh", "h", "z") for u in (FIRST, SECOND)) + (
    (("h", THIRD), ("hh", THIRD)),
    (("z", THIRD),),
    (("h", FOURTH), ("hh", FOURTH), ("hh", FIFTH), ("h", FIFTH)),
    (("z", FOURTH), ("z", FIFTH)),
)
GROUPS = ((0, 1), (2, 3), (4, 5), (6, 7))

FLOPS = 2 * B * K * (K + 8 * H + 4 * H)


def tile_hyperlstmgeneratedscalebiasstep_w8_kernel(
    tc, hh_bytes, hh_scale, h, c, wz_words, wz_scales, bz, wd_words, wd_scales, wh_words, wh_scales, out_0, out_1
):
    nc = tc.nc

    def rows_of(x):
        return x.rearrange("(p t) n -> p t n", t=TILES)

    def words_of(w):
        return w[0].rearrange("p n t -> p (n t)").bitcast(I32)

    with ExitStack() as ctx:
        keep = ctx.enter_context(tc.tile_pool(name="keep", bufs=1))
        work = ctx.enter_context(tc.tile_pool(name="work", bufs=2))
        psum = ctx.enter_context(tc.psum_pool(name="psum", bufs=2))
        ctx.enter_context(tc.manual_schedule())

        def bank(role):
            return psum.tile([P, 512], F32, name=role)

        hh_first = keep.tile([P, 2 * K], U8, name="hh_first")
        hh_rest = keep.tile([P, (TILES - 2) * K], U8, name="hh_rest")
        h_sb = {pair: keep.tile([P, 2 * K], BF16, name="h_sb%d" % pair[0]) for pair in PAIRS_IN}

        def loaded_h(u):
            j = u[0] % 2
            return h_sb[PAIRS_IN[u[0] // 2]][:, K * j : K * (j + len(u))]

        def loaded_hh(u):
            src, j = (hh_first, u[0]) if u[0] < 2 else (hh_rest, u[0] - 2)
            return src[:, K * j : K * (j + len(u))].bitcast(FP8)

        c_sb = {grp: keep.tile([P, len(grp) * H], BF16, name="c_sb%d" % grp[0]) for grp in GROUPS}
        staging, codes_of, scales_of, batch_tiles = {}, {}, {}, {}
        for b, batch in enumerate(BATCHES):
            tiles_in = sum(len(u) for name, u in batch)
            values = keep.tile([P, tiles_in * K], BF16, name="values%d" % b, align_bytes=64)
            codes = keep.tile([P, tiles_in * P], U32, name="codes%d" % b, align_bytes=64)
            scales = keep.tile([P, tiles_in * P], U8, name="scales%d" % b, align_bytes=64)
            batch_tiles[batch] = (values, codes, scales)
            at = 0
            for name, u in batch:
                staging[name, u] = values[:, K * at : K * (at + len(u))]
                for tile in u:
                    codes_of[name, tile] = codes[:, P * at : P * (at + 1)].bitcast(FP8X4)
                    scales_of[name, tile] = scales[:, P * at : P * (at + 1)]
                    at += 1
        group_of = {tile: grp for grp in GROUPS for tile in grp}
        wz_raw = keep.tile([P, K], U32, name="wz_raw")
        wz_raw_sc = keep.tile([P, K], U8, name="wz_raw_sc")
        wz = keep.tile([P, K], U32, name="wz", align_bytes=64)
        wz_sc = keep.tile([P, K], U8, name="wz_sc", align_bytes=64)
        wh = [keep.tile([P, H], U32, name="wh%d" % g, align_bytes=64) for g in range(4)]
        wd = [keep.tile([P, 2, H], U32, name="wd%d" % g, align_bytes=64) for g in range(4)]
        wh_sc = keep.tile([P, H], U8, name="wh_sc", align_bytes=64)
        wd_sc = keep.tile([P, 2 * H], U8, name="wd_sc", align_bytes=64)
        hs = keep.tile([P, 4], F32, name="hs")
        bz_sb = keep.tile([P, 4], BF16, name="bz_sb")
        hs_row = keep.tile([P, K], F32, name="hs_row")
        warm = keep.tile([P, 1], F32, name="warm")
        idle = keep.tile([P, H], BF16, name="idle")
        ident = keep.tile([P, P], F32, name="ident")

        nc.vector.memset(warm[:], 0.0)
        nc.scalar.activation(out=warm[:], in_=warm[:], func=ACT.Sigmoid)
        nc.vector.memset(wz_raw_sc[:].bitcast(I32), 0)
        nc.vector.memset(idle[:].bitcast(I32), 0)
        nc.vector.memset(wh_sc[:].bitcast(I32), 0)
        nc.vector.memset(wd_sc[:].bitcast(I32), 0)
        nc.vector.memset(ident[:], 0.0)
        nc.gpsimd.dma_start(out=bz_sb[:], in_=bz.rearrange("(p t) -> p t", t=4))
        make_identity(nc, ident[:], nomemset=True)

        def rows(x, tiles):
            return rows_of(x)[:, tiles[0] : tiles[-1] + 1, :].rearrange("p t n -> p (t n)")

        def load_rows(dst, src, u):
            nc.sync.dma_start(out=dst[u][:], in_=rows(src, u))

        def load_scales(dst, src, planes):
            scale_rows = src[0].bitcast(I32)
            for quad in range(4):
                nc.sync.dma_start(
                    out=dst[32 * quad : 32 * quad + 4 * planes, :].bitcast(I32),
                    in_=scale_rows[4 * quad : 4 * quad + 4, :].rearrange("r (c n) -> c r n", c=planes),
                )

        def load_gate(g):
            nc.sync.dma_start(out=wh[g][:].bitcast(I32), in_=words_of(wh_words)[:, H * g : H * (g + 1)])
            both = words_of(wd_words).rearrange("p (a g n) -> p a g n", a=2, g=4)
            nc.sync.dma_start(out=wd[g][:].bitcast(I32), in_=both[:, :, g, :])

        nc.sync.dma_start(out=hh_first[:], in_=rows(hh_bytes, PAIRS_IN[0]))
        nc.sync.dma_start(out=hs[:], in_=hh_scale.rearrange("o (p t) -> p (o t)", t=4))
        nc.sync.dma_start(out=wz_raw[:].bitcast(I32), in_=words_of(wz_words))
        load_scales(wz_raw_sc, wz_scales, 1)
        load_rows(h_sb, h, PAIRS_IN[0])
        nc.sync.dma_start(out=hh_rest[:], in_=rows(hh_bytes, range(2, TILES)))
        load_scales(wh_sc, wh_scales, 4)
        load_scales(wd_sc, wd_scales, 4)
        load_rows(h_sb, h, PAIRS_IN[1])
        load_gate(GATE_ORDER[0])
        load_gate(GATE_ORDER[1])
        load_rows(h_sb, h, PAIRS_IN[2])
        load_gate(GATE_ORDER[2])
        load_rows(c_sb, c, GROUPS[0])
        load_rows(h_sb, h, PAIRS_IN[3])
        load_gate(GATE_ORDER[3])
        for grp in GROUPS[1:]:
            load_rows(c_sb, c, grp)

        staged = {}

        def keep_clock(count):
            unread = bank("r_bank")
            for rep in range(count):
                nc.tensor.matmul(unread[:], lhsT=idle[:, :P], rhs=idle[:], start=True, stop=True)

        def spread(column_tile, row_tile):
            src = bank("prep")
            for t in range(4):
                nc.tensor.transpose(
                    src[:, P * t : P * (t + 1)], column_tile[:, t : t + 1].to_broadcast([P, P]), ident[:]
                )
            nc.scalar.copy(
                out=row_tile[:].rearrange("p (n t) -> p n t", t=4), in_=src[:].rearrange("p (t n) -> p n t", t=4)
            )

        def over_tiles(row_tile, u):
            return row_tile[:].unsqueeze(1).to_broadcast([P, len(u), K])

        def widen_hh(u, copy):
            wide = work.tile([P, len(u) * K], BF16, name="hh_wide", bufs=3)
            copy(out=wide[:], in_=loaded_hh(u))
            staged["hh_wide", u] = wide[:]

        def scale_rows(u, eng, src):
            dst = work.tile([P, len(u) * K], BF16, name="hh_rows")
            eng.tensor_tensor(
                out=dst[:].rearrange("p (j k) -> p j k", k=K),
                in0=src.rearrange("p (j k) -> p j k", k=K),
                in1=over_tiles(hs_row, u),
                op=ALU.mult,
            )
            staged["hh_rows", u] = dst[:]

        def turn(name, u, role="prep"):
            words = staged[name, u].bitcast(F32)
            dst = bank(role)
            for half in range(2):
                for j in range(len(u)):
                    col = P * (len(u) * half + j)
                    nc.tensor.transpose(dst[:, col : col + P], words[:, 256 * j + half : 256 * (j + 1) : 2], ident[:])
            return dst[:, : 2 * P * len(u)]

        def copy_turned(name, u, src):
            nc.scalar.copy(
                out=staging[name, u].bitcast(F32).rearrange("p (n a) -> p n a", a=2),
                in_=src.rearrange("p (a n) -> p n a", a=2),
            )

        def scale_turned(u, src):
            nc.vector.tensor_tensor(
                out=staging["hh", u].rearrange("p (n a e) -> p n a e", a=2, e=2),
                in0=src.bitcast(BF16).rearrange("p (a n e) -> p n a e", a=2, e=2),
                in1=hs[:].rearrange("p (a e) -> p a e", a=2).unsqueeze(1).to_broadcast([P, len(u) * P, 2, 2]),
                op=ALU.mult,
            )

        def quantize(*batch):
            values, codes, scales = batch_tiles[batch]
            nc.vector.quantize_mx(out=codes[:].bitcast(FP8X4), scales=scales[:], in_=values[:])

        def multiply_z(u, j):
            dst = bank("prep")
            for t in range(4):
                chans = slice(P * t, P * (t + 1))
                nc.tensor.matmul_mx(
                    out=dst[:, chans],
                    lhsT=wz[:, chans].bitcast(FP8X4),
                    lhsT_scale=wz_sc[:, chans],
                    rhs=codes_of["hh", u[j]],
                    rhs_scale=scales_of["hh", u[j]],
                    start=True,
                    stop=True,
                )
            staged["z_bank", u, j] = dst

        def bias_z(u, j):
            nc.vector.tensor_tensor(
                out=staging["z", u][:, K * j : K * (j + 1)].rearrange("p (n t) -> p n t", t=4),
                in0=staged["z_bank", u, j][:].rearrange("p (t n) -> p n t", t=4),
                in1=bz_sb[:].unsqueeze(1).to_broadcast([P, P, 4]),
                op=ALU.add,
            )

        for u in UNITS:
            staged["h_rows", u] = loaded_h(u)

        chunks = [(tile, g) for grp in GROUPS for g in GATE_ORDER for tile in grp]

        def gate_matmul(role, name, tile, weights, weight_scales):
            dst = bank(role)
            nc.tensor.matmul_mx(
                out=dst[:],
                lhsT=codes_of[name, tile],
                lhsT_scale=scales_of[name, tile],
                rhs=weights.bitcast(FP8X4),
                rhs_scale=weight_scales,
                start=True,
                stop=True,
            )
            return dst

        def wd_scales_of(first_col):
            plane, col = divmod(first_col, 2 * H)
            return wd_sc[4 * plane :, col : col + H]

        def recurrent(n, role="r_bank"):
            tile, g = chunks[n]
            src = gate_matmul(role, "h", tile, wh[g][:], wh_sc[4 * g :, :])
            r = work.tile([P, H], F32, name="r", bufs=R_AHEAD + 4)
            nc.scalar.copy(out=r[:], in_=src[:])
            staged["r", n] = r

        def pre_slice(n):
            tile, g = chunks[n]
            grp = group_of[tile]
            if ("pre", grp, g) not in staged:
                staged["pre", grp, g] = work.tile([P, len(grp) * H], F32, name="pre", bufs=4)
            j = tile - grp[0]
            return staged["pre", grp, g][:, H * j : H * (j + 1)]

        def multiply_d(n):
            tile, g = chunks[n]
            staged["d", n] = gate_matmul("d_bank", "z", tile, wd[g][:, 0, :], wd_scales_of(H * g))

        def modulate(n):
            d = staged["d", n]
            nc.vector.scalar_tensor_tensor(
                out=pre_slice(n), in0=d[:], scalar=1.0, in1=staged["r", n][:], op0=ALU.add, op1=ALU.mult
            )

        def multiply_beta(n):
            tile, g = chunks[n]
            staged["beta", n] = gate_matmul(
                "beta_bank", "z", tile, wd[g][:, 1, :], wd_scales_of(4 * H + H * g)
            )

        def shift(n):
            tile, g = chunks[n]
            beta = staged["beta", n]
            if g == GATE_F:
                nc.vector.scalar_tensor_tensor(
                    out=pre_slice(n), in0=beta[:], scalar=1.0, in1=pre_slice(n), op0=ALU.add, op1=ALU.add
                )
            else:
                nc.vector.tensor_tensor(out=pre_slice(n), in0=beta[:], in1=pre_slice(n), op=ALU.add)

        def span(grp, part):
            return slice(H * (part[0] - grp[0]), H * (part[-1] - grp[0] + 1))

        def shared(name, grp):
            if (name, grp) not in staged:
                staged[name, grp] = work.tile([P, len(grp) * H], F32, name=name)
            return staged[name, grp]

        def activate(grp, g, part):
            cols = span(grp, part)
            nc.scalar.activation(
                out=shared("gate%d" % g, grp)[:, cols],
                in_=staged["pre", grp, g][:, cols],
                func=ACT.Tanh if g == GATE_G else ACT.Sigmoid,
            )

        def forget(grp, eng):
            eng.tensor_tensor(
                out=shared("kept", grp)[:], in0=shared("gate%d" % GATE_F, grp)[:], in1=c_sb[grp][:], op=ALU.mult
            )

        def candidate(grp, part, eng):
            cols = span(grp, part)
            gate = shared("gate%d" % GATE_G, grp)[:, cols]
            eng.tensor_tensor(out=gate, in0=gate, in1=shared("gate%d" % GATE_I, grp)[:, cols], op=ALU.mult)

        def cell(grp, part, eng):
            cols = span(grp, part)
            c1 = shared("c1", grp)[:, cols]
            eng.tensor_tensor(
                out=c1, in0=shared("gate%d" % GATE_G, grp)[:, cols], in1=shared("kept", grp)[:, cols], op=ALU.add
            )
            nc.sync.dma_start(out=rows(out_1, part), in_=c1)

        def squash(grp, part):
            cols = span(grp, part)
            nc.scalar.activation(out=shared("squashed", grp)[:, cols], in_=shared("c1", grp)[:, cols], func=ACT.Tanh)

        def hidden(grp, part, eng):
            cols = span(grp, part)
            h1 = shared("h1", grp)[:, cols]
            eng.tensor_tensor(
                out=h1, in0=shared("squashed", grp)[:, cols], in1=shared("gate%d" % GATE_O, grp)[:, cols], op=ALU.mult
            )
            nc.sync.dma_start(out=rows(out_0, part), in_=h1)

        first, second, third, fourth, fifth = UNITS
        keep_clock(4)
        widen_hh(first, nc.vector.tensor_copy)
        widen_hh(second, nc.scalar.copy)
        hh_bank = [turn("hh_wide", u, "d_bank") for u in (first, second)]
        nc.vector.tensor_copy(
            out=wz[:].bitcast(I32).rearrange("p (t m) -> p t m", t=4),
            in_=wz_raw[:].bitcast(I32).rearrange("p (m t) -> p t m", t=4),
        )
        scale_turned(first, hh_bank[0])
        nc.vector.tensor_copy(
            out=wz_sc[:].rearrange("p (t m) -> p t m", t=4), in_=wz_raw_sc[:].rearrange("p (m t) -> p t m", t=4)
        )
        copy_turned("h", first, turn("h_rows", first, "beta_bank"))
        keep_clock(2)
        widen_hh(third, nc.scalar.copy)
        quantize(("hh", first))
        scale_turned(second, hh_bank[1])
        multiply_z(first, 0)
        keep_clock(1)
        copy_turned("h", second, turn("h_rows", second, "beta_bank"))
        quantize(("hh", second))
        bias_z(first, 0)
        multiply_z(second, 0)
        keep_clock(1)
        third_bank = turn("hh_wide", third, "d_bank")
        widen_hh(fourth, nc.scalar.copy)
        copy_turned("h", third, turn("h_rows", third, "beta_bank"))
        quantize(("h", first))
        bias_z(second, 0)
        quantize(("z", first))
        quantize(("h", second))
        recurrent(0)
        recurrent(1)
        quantize(("z", second))
        scale_turned(third, third_bank)
        multiply_d(0)
        modulate(0)
        quantize(*BATCHES[-4])
        multiply_d(1)
        modulate(1)
        recurrent(2)
        spread(hs, hs_row)
        scale_rows(fourth, nc.gpsimd, staged["hh_wide", fourth])

        last = len(chunks) - 1
        done_at = {}
        for n, (tile, g) in enumerate(chunks):
            done_at[group_of[tile], g] = n
        final = GROUPS[-1]
        parts = [(tile,) for tile in final]
        recurrent_next = 3
        for n in range(len(chunks)):
            if n - 1 in SLOTS:
                multiply_beta(n)
                shift(n)
            if n + 2 <= last:
                multiply_d(n + 2)
                modulate(n + 2)
            if n - 1 not in SLOTS:
                multiply_beta(n)
                shift(n)
            for grp in GROUPS:
                if done_at[grp, GATE_F] == n - 1:
                    activate(grp, GATE_F, grp)
                    forget(grp, nc.gpsimd)
                if done_at[grp, GATE_I] == n - 1:
                    activate(grp, GATE_I, grp)
                if done_at[grp, GATE_G] == n - 1:
                    activate(grp, GATE_G, grp)
                    if grp != final:
                        candidate(grp, grp, nc.gpsimd)
                        cell(grp, grp, nc.gpsimd)
                if done_at[grp, GATE_O] == n - 1:
                    activate(grp, GATE_O, grp)
            for step in range(2):
                if recurrent_next <= min(last, n + R_AHEAD + (2 if n >= 12 else 0)) and (step == 0 or n >= RAMP):
                    recurrent(recurrent_next, "prep" if n >= 12 and recurrent_next % 2 else "r_bank")
                    recurrent_next += 1
            if n == WF:
                widen_hh(fifth, nc.scalar.copy)
                scale_rows(fifth, nc.gpsimd, staged["hh_wide", fifth])
            for grp in GROUPS[:2]:
                if done_at[grp, GATE_G] + TANH_LAG == n:
                    squash(grp, grp)
                    hidden(grp, grp, nc.gpsimd)
            if n == last - 2:
                squash(GROUPS[2], GROUPS[2])
            for u, start in ((third, 0), (fourth, 7), (fifth, 9)):
                if n - start in (0, 1):
                    multiply_z(u, n - start)
                if n - start in (1, 2):
                    bias_z(u, n - start - 1)
            if n == 2:
                copy_turned("h", fourth, turn("h_rows", fourth))
            if n == 3:
                copy_turned("hh", fourth, turn("hh_rows", fourth))
            if n == 4:
                copy_turned("hh", fifth, turn("hh_rows", fifth))
            if n == 5:
                quantize(*BATCHES[-3])
                quantize(*BATCHES[-2])
            if n == THF:
                copy_turned("h", fifth, turn("h_rows", fifth))
            if n == 13:
                quantize(*BATCHES[-1])

        hidden(GROUPS[2], GROUPS[2], nc.vector)
        for part in parts:
            activate(final, GATE_O, part)
            candidate(final, part, nc.vector)
        for part in parts:
            cell(final, part, nc.vector)
            squash(final, part)
        for part in parts:
            hidden(final, part, nc.vector)
